import numpy as np
import ml_dtypes


def mxq(x, axis, fmt="e4m3"):
    dtype, down = {"e4m3": (ml_dtypes.float8_e4m3fn, 7), "e5m2": (ml_dtypes.float8_e5m2, 14)}[fmt]
    v = np.moveaxis(np.asarray(x, np.float32).astype(ml_dtypes.bfloat16).astype(np.float64), axis, -1)
    blocks = v.reshape(v.shape[:-1] + (-1, 32))
    amax = np.abs(blocks).max(-1, keepdims=True)
    byte = np.maximum(np.where(amax > 0, np.frexp(amax)[1] - 1 + 127, 0) - down, 1)
    scale = np.exp2(byte - 127.0)
    codes = (blocks / scale).astype(np.float32).astype(dtype).astype(np.float64)
    return np.moveaxis((codes * scale).reshape(v.shape), -1, axis)


WIDE = False


def mx_kscale(k):
    if not WIDE:
        return np.ones(k)
    levels = np.array([10, -10, 5, -5, 0])
    if k % 512:
        return np.exp2(np.random.permutation(np.resize(levels, k // 32))).repeat(32)
    a = np.empty((k // 512, 16))
    for p in range(k // 512):
        a[p, :8] = np.random.permutation(np.resize(levels, 8))
        for g in range(8):
            far = levels[np.abs(levels - a[p, g]) >= 10]
            a[p, g + 8] = far[np.random.randint(len(far))]
    return np.exp2(a.ravel()).repeat(32)


def f64(x):
    return np.asarray(x).astype(np.float64)


def striped(idx):
    return np.tile(np.asarray(idx).reshape(-1, 16).T, (8, 1)).astype(np.uint16)


def unstriped(offs):
    return offs[:16].T.reshape(-1).astype(np.int64)


B, N, T, D, DV, NQ = 2, 512, 2048, 512, 256, 128
PAGE = 64


def setup_inputs():
    n = np.random.standard_normal
    pages = np.random.permutation(T // PAGE)[:B * N // PAGE]
    idx = (pages[:, None] * PAGE + np.arange(PAGE)[None, :]).reshape(-1)
    s = mx_kscale(D)[:, None]
    u = np.ones(T)
    u[idx] = mx_kscale(B * N)
    r = np.random.uniform(0.5, 2.0, T)
    k = n((D, T)) / s
    v = n((DV, T)) / (u * r)
    return {
        "qT": (n((B, D, NQ)) * s * (1.00 / np.sqrt(D))).astype(np.float32),
        "kT": k.astype(np.float32),
        "vT": v.astype(np.float32),
        "vs": np.tile(u * r, (128, 1)).astype(np.float32),
        "og": n((B, NQ, DV)).astype(np.float32),
        "offs": striped(idx),
    }


def reference(qT, kT, vT, vs, og, offs):
    idx = unstriped(offs)
    k = f64(kT)
    v = f64(vT)
    pick = lambda x: x[:, idx].reshape(x.shape[0], B, N).transpose(1, 0, 2)
    q = f64(qT)
    score = mxq(q, 1, "e4m3").transpose(0, 2, 1) @ mxq(pick(k), 1, "e4m3")
    p = 1.0 / (1.0 + np.exp(-score))
    w = p * pick(f64(vs))[:, :1, :]
    y = mxq(w, 2, "e4m3") @ mxq(pick(v).transpose(0, 2, 1), 1, "e4m3")
    y = y / 16.0
    y = y / (1.0 + np.exp(-f64(og)))
    return y

from contextlib import ExitStack

import concourse.mybir as mybir
from concourse.masks import make_identity

B, N, T, D, DV, NQ = 2, 512, 2048, 512, 256, 128
P = 128
PACK = 4

F32 = mybir.dt.float32
BF16 = mybir.dt.bfloat16
U32 = mybir.dt.uint32
U16 = mybir.dt.uint16
U8 = mybir.dt.uint8
FP8X4 = mybir.dt.float8_e4m3fn_x4
SIGMOID = mybir.ActivationFunctionType.Sigmoid
MULT = mybir.AluOpType.mult

FLOPS = 2 * B * NQ * N * (D + DV)
BYTES = 4 * (B * D * NQ + D * T + DV * T + T + 2 * B * NQ * DV) + 2 * P * (B * N // 16)


def tile_attend_x_sigmoid_gate_kernel(tc, qT, kT, vT, vs, og, offs, out):
    nc = tc.nc
    cols = N // 16

    with ExitStack() as ctx:
        keep = ctx.enter_context(tc.tile_pool(name="keep", bufs=1))
        psum = ctx.enter_context(tc.psum_pool(name="psum", bufs=1))

        vs_win = keep.tile([P, T], F32, name="vs_win")
        nc.vector.memset(vs_win[:], 0.0)
        offsets = keep.tile([P, B * N // 16], U16, name="offsets")
        nc.sync.dma_start(offsets[:], offs)

        k_rows = kT.rearrange("(p j) t -> j p t", j=PACK)
        k_win = []
        for j in range(PACK):
            w = keep.tile([P, T], F32, name=f"k_win{j}")
            nc.sync.dma_start(w[:], k_rows[j])
            k_win.append(w)
            if j == 0:
                nc.sync.dma_start(vs_win[0:1, :], vs[0:1, :])
        q_raw = keep.tile([P, B, PACK * NQ], F32, name="q_raw")
        nc.sync.dma_start(q_raw[:], qT.rearrange("b (p j) q -> p b (j q)", j=PACK))
        v_win = []
        for h in range(2):
            w = keep.tile([P, T], F32, name=f"v_win{h}")
            nc.sync.dma_start(w[:], vT[h * P : (h + 1) * P, :])
            v_win.append(w)
        og_sb = keep.tile([P, B, DV], F32, name="og_sb")
        nc.sync.dma_start(og_sb[:], og.rearrange("b q e -> q b e"))

        warm = keep.tile([P, 1], F32, name="warm")
        nc.vector.memset(warm[:], 0.0)
        nc.scalar.activation(warm[:], warm[:], SIGMOID)
        ident_f = keep.tile([P, P], F32, name="ident_f")
        make_identity(nc, ident_f[:])
        ident_b = keep.tile([P, P], BF16, name="ident_b")
        make_identity(nc, ident_b[:])

        kg01 = keep.tile([P, 2, B * N], F32, name="kg01")
        kg23 = keep.tile([P, 2, B * N], F32, name="kg23")
        k_grouped = [keep.tile([P, PACK * N], BF16, name=f"k_grouped{b}", align_bytes=64) for b in range(B)]

        def k_interleave(copy, src, b, j0):
            dst = k_grouped[b][:].rearrange("p (t m j) -> p m t j", t=PACK, j=PACK)
            copy(
                out=dst[:, :, :, j0 : j0 + 2],
                in_=src[:, :, b * N : (b + 1) * N].rearrange("p j (m t) -> p m t j", t=PACK),
            )

        nc.vector.tensor_copy(kg01[:, 0, :], k_win[0][:].indirect(offsets[:]))
        nc.vector.tensor_copy(kg01[:, 1, :], k_win[1][:].indirect(offsets[:]))
        vs_picked = keep.tile([P, B * N], F32, name="vs_picked")
        nc.vector.tensor_copy(vs_picked[:], vs_win[:].indirect(offsets[:]))
        for b in range(B):
            k_interleave(nc.scalar.copy, kg01, b, 0)

        vs_col = []
        for b in range(B):
            turned = psum.tile([P, PACK, P], F32, name="turned", tag="turned_vs", bufs=1)
            picked = vs_picked[:, b * N : (b + 1) * N].rearrange("p (m t) -> p t m", t=PACK)
            for t in range(PACK):
                nc.tensor.transpose(turned[:, t, :], picked[:, t, :], ident_f[:])
            c = keep.tile([P, 1, PACK], F32, name=f"vs_col{b}")
            nc.vector.tensor_copy(out=c[:], in_=turned[:, :, 0:1].rearrange("p t o -> p o t"))
            vs_col.append(c)

        nc.vector.tensor_copy(kg23[:, 0, :], k_win[2][:].indirect(offsets[:]))

        k_codes = [keep.tile([P, N], U32, name=f"k_codes{b}", align_bytes=64) for b in range(B)]
        k_scales = [keep.tile([P, N], U8, name=f"k_scales{b}", align_bytes=64) for b in range(B)]
        q_grouped = [keep.tile([P, NQ, PACK], BF16, name=f"q_grouped{b}", align_bytes=64) for b in range(B)]
        q_codes = [keep.tile([P, NQ], U32, name=f"q_codes{b}", align_bytes=64) for b in range(B)]
        q_scales = [keep.tile([P, NQ], U8, name=f"q_scales{b}", align_bytes=64) for b in range(B)]
        p_sb = [keep.tile([P, NQ, PACK], F32, name=f"p_sb{b}") for b in range(B)]
        w_grouped = [keep.tile([P, NQ, PACK], BF16, name=f"w_grouped{b}", align_bytes=64) for b in range(B)]
        w_codes = [keep.tile([P, NQ], U32, name=f"w_codes{b}", align_bytes=64) for b in range(B)]
        w_scales = [keep.tile([P, NQ], U8, name=f"w_scales{b}", align_bytes=64) for b in range(B)]
        v_picked = [[keep.tile([P, N], BF16, name=f"v_picked{h}{b}") for b in range(B)] for h in range(2)]
        v_grouped = [[keep.tile([P, P, PACK], BF16, name=f"v_grouped{h}{b}", align_bytes=64) for b in range(B)] for h in range(2)]
        v_codes = [[keep.tile([P, P], U32, name=f"v_codes{h}{b}", align_bytes=64) for b in range(B)] for h in range(2)]
        v_scales = [[keep.tile([P, P], U8, name=f"v_scales{h}{b}", align_bytes=64) for b in range(B)] for h in range(2)]

        def quantize(codes, scales, grouped):
            nc.vector.quantize_mx(out=codes[:].bitcast(FP8X4), scales=scales[:], in_=grouped)

        def gather_k3(b):
            nc.vector.tensor_copy(
                kg23[:, 1, b * N : (b + 1) * N], k_win[3][:].indirect(offsets[:, b * cols : (b + 1) * cols])
            )

        def q_interleave(b):
            nc.scalar.copy(out=q_grouped[b][:], in_=q_raw[:, b, :].rearrange("p (j q) -> p q j", j=PACK))

        def q_quantize(b):
            quantize(q_codes[b], q_scales[b], q_grouped[b][:].rearrange("p q j -> p (q j)"))

        scores = [None, None]

        def score(b):
            bank = psum.tile([P, PACK, NQ], F32, name=f"score{b}")
            for t in range(PACK):
                c = slice(t * P, (t + 1) * P)
                nc.tensor.matmul_mx(
                    out=bank[:, t, :],
                    lhsT=k_codes[b][:, c].bitcast(FP8X4),
                    lhsT_scale=k_scales[b][:, c],
                    rhs=q_codes[b][:].bitcast(FP8X4),
                    rhs_scale=q_scales[b][:],
                    start=True,
                    stop=True,
                )
            nc.scalar.activation(p_sb[b][:], bank[:].rearrange("p t q -> p q t"), SIGMOID)

        def weights(b):
            nc.vector.tensor_tensor(
                w_grouped[b][:], p_sb[b][:], vs_col[b][:].to_broadcast([P, NQ, PACK]), MULT
            )

        def w_quantize(b):
            quantize(w_codes[b], w_scales[b], w_grouped[b][:].rearrange("p q j -> p (q j)"))

        def gather_v(h, b):
            nc.vector.tensor_copy(
                v_picked[h][b][:].rearrange("p (t m) -> p m t", t=PACK),
                v_win[h][:].indirect(offsets[:, b * cols : (b + 1) * cols]),
            )

        def turn_v(h, b):
            bank = psum.tile([P, PACK, P], BF16, name="turned", tag="turned_v", bufs=3)
            for t in range(PACK):
                nc.tensor.transpose(bank[:, t, :], v_picked[h][b][:, t * P : (t + 1) * P], ident_b[:])
            nc.scalar.copy(out=v_grouped[h][b][:], in_=bank[:].rearrange("p t e -> p e t"))

        def v_quantize(h, b):
            quantize(v_codes[h][b], v_scales[h][b], v_grouped[h][b][:].rearrange("p e t -> p (e t)"))

        y_bank = [psum.tile([P, 2, P], F32, name=f"y_bank{b}") for b in range(B)]

        def finish(h, b):
            nc.tensor.matmul_mx(
                out=y_bank[b][:, h, :],
                lhsT=w_codes[b][:].bitcast(FP8X4),
                lhsT_scale=w_scales[b][:],
                rhs=v_codes[h][b][:].bitcast(FP8X4),
                rhs_scale=v_scales[h][b][:],
                start=True,
                stop=True,
            )
            e = slice(h * P, (h + 1) * P)
            o = keep.tile([P, P], F32, name=f"o{h}{b}")
            nc.vector.scalar_tensor_tensor(o[:], y_bank[b][:, h, :], 1.0 / 16.0, gate[:, b, e], MULT, MULT)
            nc.sync.dma_start(out[b, :, e], o[:])

        gather_k3(0)
        k_interleave(nc.vector.tensor_copy, kg23, 0, 2)
        gather_k3(1)
        k_interleave(nc.scalar.copy, kg23, 1, 2)
        quantize(k_codes[0], k_scales[0], k_grouped[0][:])
        for b in range(B):
            q_interleave(b)
        for b in range(B):
            q_quantize(b)
        score(0)
        quantize(k_codes[1], k_scales[1], k_grouped[1][:])
        score(1)
        gather_v(0, 0)
        turn_v(0, 0)
        gather_v(0, 1)
        turn_v(0, 1)
        weights(0)
        w_quantize(0)
        weights(1)
        w_quantize(1)
        v_quantize(0, 0)
        v_quantize(0, 1)
        gate = keep.tile([P, B, DV], F32, name="gate")
        gather_v(1, 0)
        turn_v(1, 0)
        nc.scalar.activation(gate[:], og_sb[:], SIGMOID)
        finish(0, 0)
        finish(0, 1)
        gather_v(1, 1)
        turn_v(1, 1)
        v_quantize(1, 0)
        finish(1, 0)
        v_quantize(1, 1)
        finish(1, 1)
